import numpy as np
import ml_dtypes


def mxq(x, axis, fmt="e4m3"):
    dtype, down = {"e4m3": (ml_dtypes.float8_e4m3fn, 7), "e5m2": (ml_dtypes.float8_e5m2, 14)}[fmt]
    v = np.moveaxis(np.asarray(x, np.float32).astype(ml_dtypes.bfloat16).astype(np.float64), axis, -1)
    blocks = v.reshape(v.shape[:-1] + (-1, 32))
    amax = np.abs(blocks).max(-1, keepdims=True)
    byte = np.maximum(np.where(amax > 0, np.frexp(amax)[1] - 1 + 127, 0) - down, 1)
    scale = np.exp2(byte - 127.0)
    codes = (blocks / scale).astype(np.float32).astype(dtype).astype(np.float64)
    return np.moveaxis((codes * scale).reshape(v.shape), -1, axis)


WIDE = False


def mx_kscale(k):
    if not WIDE:
        return np.ones(k)
    levels = np.array([10, -10, 5, -5, 0])
    if k % 512:
        return np.exp2(np.random.permutation(np.resize(levels, k // 32))).repeat(32)
    a = np.empty((k // 512, 16))
    for p in range(k // 512):
        a[p, :8] = np.random.permutation(np.resize(levels, 8))
        for g in range(8):
            far = levels[np.abs(levels - a[p, g]) >= 10]
            a[p, g + 8] = far[np.random.randint(len(far))]
    return np.exp2(a.ravel()).repeat(32)


def f64(x):
    return np.asarray(x).astype(np.float64)


def striped(idx):
    return np.tile(idx.reshape(-1, 16).T, (8, 1)).astype(np.uint16)


def unstriped(offs):
    return offs[:16].T.reshape(-1).astype(np.int64)


E2M1 = np.array([0.0, 0.5, 1.0, 1.5, 2.0, 3.0, 4.0, 6.0, -0.0, -0.5, -1.0, -1.5, -2.0, -3.0, -4.0, -6.0])


def pack_weight(w, fmt):
    k, n = w.shape
    w = f64(np.asarray(w, np.float32).astype(ml_dtypes.bfloat16)).reshape(k // 32, 32, n)
    amax = np.abs(w).max(1)
    if fmt == "e4m3":
        byte = np.frexp(amax)[1] - 1 + 127 - 7
    else:
        mant, ex = np.frexp(amax / 6.0)
        byte = np.where(mant > 0.5, ex, ex - 1) + 127
    byte = np.clip(np.where(amax > 0, byte, 1), 1, 254)
    scaled = (w * np.exp2(127.0 - byte)[:, None, :]).reshape(k, n).astype(np.float32)
    by_word = np.ascontiguousarray(scaled.reshape(k // 512, 128, 4, n).transpose(0, 1, 3, 2))
    if fmt == "e4m3":
        words = by_word.astype(ml_dtypes.float8_e4m3fn).view(np.uint8)
    else:
        c = by_word.astype(ml_dtypes.float4_e2m1fn).view(np.uint8) & 0xF
        words = (c[..., 0::2] | (c[..., 1::2] << 4)).reshape(k // 512, 128, 2 * n)
    return np.ascontiguousarray(words), np.ascontiguousarray(byte.astype(np.uint8).reshape(k // 512, 16, n))


def unpack_weight(words, scales, fmt):
    g, _, n = scales.shape
    words = np.ascontiguousarray(words).reshape(g, 128, n, -1)
    if fmt == "e4m3":
        vals = words.view(ml_dtypes.float8_e4m3fn).astype(np.float64)
    else:
        nib = np.empty((g, 128, n, 4), np.uint8)
        nib[..., 0::2] = words & 0xF
        nib[..., 1::2] = words >> 4
        vals = E2M1[nib]
    vals = vals * np.repeat(np.exp2(scales.astype(np.float64) - 127.0), 8, axis=1)[..., None]
    return vals.transpose(0, 1, 3, 2).reshape(g * 512, n)


K, T, E, C, N = 1024, 768, 4, 256, 128
PAD = 32
K8 = 512


def by_expert(wq, xq):
    return np.concatenate([wq[e].T @ xq[:, e * C:(e + 1) * C] for e in range(E)], axis=1)


def setup_inputs():
    n = np.random.standard_normal
    s = mx_kscale(K)[:, None]
    first = np.random.permutation(np.repeat(np.arange(E), T // E))
    second = (first + 1 + np.random.permutation(np.repeat(np.arange(E - 1), -(-T // (E - 1)))[:T])) % E
    while np.bincount(second, minlength=E).max() != T // E:
        load = np.bincount(second, minlength=E); hi, lo = int(load.argmax()), int(load.argmin())
        t = np.flatnonzero((second == hi) & (first != lo))[0]; second[t] = lo
    slot_token = np.empty(E * C, np.int64); pos = np.empty((2, T), np.int64); fill = np.zeros(E, np.int64)
    place = np.stack([np.random.permutation(C) for _ in range(E)])
    for r, deal in enumerate((first, second)):
        for t in np.random.permutation(T):
            e = deal[t]
            if fill[e] < C: j = e * C + place[e, fill[e]]; fill[e] += 1; slot_token[j] = t; pos[r, t] = j
            else: pos[r, t] = E * C + t % PAD
    g = np.random.uniform(0.2, 0.8, T)
    w = n((E, K, N)) / np.sqrt(K) / s[None]
    w8 = [pack_weight(m[:K8], "e4m3") for m in w]
    w4 = [pack_weight(m[K8:], "e2m1") for m in w]
    return {
        "xT": (n((K, T)) * s).astype(np.float32),
        "w8_words": np.stack([m[0] for m in w8]),
        "w8_scales": np.stack([m[1] for m in w8]),
        "w4_words": np.stack([m[0] for m in w4]),
        "w4_scales": np.stack([m[1] for m in w4]),
        "b": (0.3 * n((N, E))).astype(np.float32),
        "gate": np.stack([np.tile(g, (N, 1)), np.tile(1.0 - g, (N, 1))]).astype(np.float32),
        "offs": striped(slot_token),
        "pos1": striped(pos[0]),
        "pos2": striped(pos[1]),
    }


def reference(xT, w8_words, w8_scales, w4_words, w4_scales, b, gate, offs, pos1, pos2):
    idx = unstriped(offs)
    w = np.stack([np.concatenate([unpack_weight(w8_words[e], w8_scales[e], "e4m3"), unpack_weight(w4_words[e], w4_scales[e], "e2m1")]) for e in range(E)])
    xq = mxq(f64(xT)[:, idx], 0, "e4m3")
    y = by_expert(w, xq)
    y = y + np.repeat(f64(b), C, axis=1)
    y = np.concatenate([y, np.zeros((N, PAD))], axis=1)
    return f64(gate[0]) * y[:, unstriped(pos1)] + f64(gate[1]) * y[:, unstriped(pos2)]

@@ -1,0 +1,174 @@
+from contextlib import ExitStack
+
+import concourse.mybir as mybir
+
+K, T, E, C, N = 1024, 768, 4, 256, 128
+PAD = 32
+P = 128
+PACK = 4
+SLOTS = E * C
+FLOPS = 2 * K * N * SLOTS
+
+F32 = mybir.dt.float32
+BF16 = mybir.dt.bfloat16
+I32 = mybir.dt.int32
+U32 = mybir.dt.uint32
+U16 = mybir.dt.uint16
+U8 = mybir.dt.uint8
+E4M3X4 = mybir.dt.float8_e4m3fn_x4
+E2M1X4 = mybir.dt.float4_e2m1fn_x4
+
+MULT = mybir.AluOpType.mult
+ADD = mybir.AluOpType.add
+IDENTITY = mybir.ActivationFunctionType.Identity
+
+CHUNKS = (
+    (0, 0, 512, 352),
+    (0, 512, 256, 176),
+    (1, 0, 256, 0),
+    (1, 256, 256, 0),
+    (1, 512, 256, 96),
+)
+SCALE_ROW = (4, 0)
+
+
+def tile_moe_cap2_lin_bias_kernel(
+    tc, xT, w8_words, w8_scales, w4_words, w4_scales, b, gate, offs, pos1, pos2, out
+):
+    nc = tc.nc
+    with ExitStack() as ctx:
+        lists = ctx.enter_context(tc.tile_pool(name="lists", bufs=1))
+        keep = ctx.enter_context(tc.tile_pool(name="keep", bufs=1))
+        psum = ctx.enter_context(tc.psum_pool(name="psum", bufs=1))
+
+        offs_sb = lists.tile([P, SLOTS // 16], U16, name="offs_sb")
+        pos1_sb = lists.tile([P, T // 16], U16, name="pos1_sb")
+        pos2_sb = lists.tile([P, T // 16], U16, name="pos2_sb")
+
+        s8 = keep.tile([P, E * N], U8, align_bytes=64, name="s8")
+        s4 = keep.tile([P, E * N], U8, align_bytes=64, name="s4")
+        nc.vector.memset(s8[:].bitcast(I32), 0)
+        nc.vector.memset(s4[:].bitcast(I32), 0)
+        token_bytes = keep.tile([P, T], U8, align_bytes=64, name="token_bytes")
+        nc.vector.memset(token_bytes[:].bitcast(I32), 0)
+        y = keep.tile([P, SLOTS + PAD], F32, align_bytes=64, name="y")
+        nc.vector.memset(y[:, SLOTS:], 0.0)
+
+        for plane, scales, queue in ((s8, w8_scales, nc.gpsimd), (s4, w4_scales, nc.gpsimd)):
+            view = plane[:].rearrange("p (e n) -> p e n", e=E)
+            for q in range(4):
+                queue.dma_start(
+                    out=view[32 * q : 32 * q + 4, :, :].bitcast(I32),
+                    in_=scales[:, 0, 4 * q : 4 * q + 4, :].rearrange("e q n -> q e n").bitcast(I32),
+                )
+
+        raws = []
+        for i, (a, t0, n, v) in enumerate(CHUNKS):
+            raw = keep.tile([P, PACK, n], F32, align_bytes=64, name="raw%d" % i)
+            rows = xT[a * 512 : (a + 1) * 512, t0 : t0 + n]
+            nc.sync.dma_start(out=raw[:], in_=rows.rearrange("(p j) t -> p j t", j=PACK))
+            raws.append(raw)
+            if i == 1:
+                nc.sync.dma_start(offs_sb[:], offs)
+
+        w8 = keep.tile([P, E, 4 * N], U8, align_bytes=64, name="w8")
+        nc.sync.dma_start(out=w8[:].bitcast(I32), in_=w8_words[:, 0].rearrange("e p n r -> p e (n r)").bitcast(I32))
+        w4 = keep.tile([P, E, 2 * N], U8, align_bytes=64, name="w4")
+        nc.sync.dma_start(out=w4[:].bitcast(I32), in_=w4_words[:, 0].rearrange("e p n -> p e n").bitcast(I32))
+        bias = keep.tile([P, E], F32, name="bias")
+        nc.sync.dma_start(out=bias[:], in_=b)
+        nc.sync.dma_start(pos1_sb[:], pos1)
+        nc.sync.dma_start(pos2_sb[:], pos2)
+        gates = keep.tile([P, 2, T], F32, align_bytes=64, name="gates")
+        nc.sync.dma_start(out=gates[:], in_=gate.rearrange("a p t -> p a t"))
+
+        words = [keep.tile([P, T], U32, align_bytes=64, name="words%d" % a) for a in range(2)]
+        slot_words = [keep.tile([P, SLOTS], U32, align_bytes=64, name="slot_words%d" % a) for a in range(2)]
+        slot_bytes = keep.tile([P, SLOTS], U8, align_bytes=64, name="slot_bytes")
+
+        grouped = [keep.tile([P, T, PACK], BF16, align_bytes=64, name="grouped%d" % a) for a in range(2)]
+
+        def cast(i):
+            a, t0, n, v = CHUNKS[i]
+            for copy, c0, c1 in ((nc.vector.tensor_copy, 0, v), (nc.scalar.copy, v, n)):
+                if c0 < c1:
+                    copy(
+                        grouped[a][:, t0 + c0 : t0 + c1, :].rearrange("p (c i) j -> p c j i", i=4),
+                        raws[i][:, :, c0:c1].rearrange("p j (c i) -> p c j i", i=4),
+                    )
+
+        def quantise(a, t0, n):
+            nc.vector.quantize_mx(
+                out=words[a][:, t0 : t0 + n].bitcast(E4M3X4),
+                scales=token_bytes[SCALE_ROW[a] : P, t0 : t0 + n],
+                in_=grouped[a][:, t0 : t0 + n, :].rearrange("p t j -> p (t j)"),
+            )
+
+        def gather(dst, src, s0, n):
+            nc.vector.tensor_copy(dst[:, s0 : s0 + n], src[:].indirect(offs_sb[:, s0 // 16 : (s0 + n) // 16]))
+
+        cast(0)
+        quantise(0, 0, 512)
+        cast(1)
+        quantise(0, 512, 256)
+        gather(slot_words[0], words[0], 0, 512)
+        cast(2)
+        gather(slot_words[0], words[0], 512, 384)
+        cast(3)
+        quantise(1, 0, 256)
+        cast(4)
+        quantise(1, 256, 256)
+        quantise(1, 512, 256)
+        gather(slot_words[0], words[0], 896, 128)
+
+        banks = [psum.tile([P, 128], F32, name="bank%d" % i) for i in range(SLOTS // 128)]
+
+        def multiply(a, i):
+            s0 = 128 * i
+            e = s0 // C
+            nc.tensor.matmul_mx(
+                out=banks[i][:],
+                lhsT=(w8[:, e, :].bitcast(E4M3X4), w4[:, e, :].bitcast(E2M1X4))[a],
+                lhsT_scale=(s8, s4)[a][:, e * N : (e + 1) * N],
+                rhs=slot_words[a][:, s0 : s0 + 128].bitcast(E4M3X4),
+                rhs_scale=slot_bytes[SCALE_ROW[a] : P, s0 : s0 + 128],
+                start=(a == 0),
+                stop=(a == 1),
+            )
+
+        for s0 in (0, 512):
+            gather(slot_bytes, token_bytes, s0, 512)
+            for i in range(s0 // 128, s0 // 128 + 4):
+                multiply(0, i)
+
+        for s0, n in ((0, 512), (512, 384), (896, 128)):
+            gather(slot_words[1], words[1], s0, n)
+            for i in range(s0 // 128, (s0 + n) // 128):
+                multiply(1, i)
+                e = i // 2
+                cols = slice(128 * i, 128 * i + 128)
+                if i != 6:
+                    nc.scalar.activation(y[:, cols], banks[i][:], IDENTITY, bias=bias[:, e : e + 1], scale=1.0)
+                else:
+                    nc.vector.tensor_scalar(y[:, cols], banks[i][:], bias[:, e : e + 1], None, ADD)
+
+        first = keep.tile([P, T], F32, align_bytes=64, name="first")
+        second = keep.tile([P, T], F32, align_bytes=64, name="second")
+        result = keep.tile([P, T], F32, align_bytes=64, name="result")
+
+        def weigh(target, which, entries_sb, t0, n):
+            cols = slice(t0, t0 + n)
+            nc.vector.tensor_tensor(target[:, cols], y[:].indirect(entries_sb[:, t0 // 16 : (t0 + n) // 16]), gates[:, which, cols], MULT)
+
+        def finish(t0, n):
+            cols = slice(t0, t0 + n)
+            nc.vector.tensor_tensor(result[:, cols], first[:, cols], second[:, cols], ADD)
+            nc.sync.dma_start(out=out[:, cols], in_=result[:, cols])
+
+        weigh(first, 0, pos1_sb, 0, 512)
+        weigh(second, 1, pos2_sb, 0, 512)
+        weigh(first, 0, pos1_sb, 512, 256)
+        finish(0, 256)
+        weigh(second, 1, pos2_sb, 512, 256)
+        finish(256, 256)
+        finish(512, 256)

@@ -23,11 +23,12 @@ ADD = mybir.AluOpType.add
 IDENTITY = mybir.ActivationFunctionType.Identity
 
 CHUNKS = (
-    (0, 0, 512, 352),
-    (0, 512, 256, 176),
+    (0, 0, 256, 160),
+    (0, 256, 256, 160),
+    (0, 512, 256, 160),
     (1, 0, 256, 0),
     (1, 256, 256, 0),
-    (1, 512, 256, 96),
+    (1, 512, 256, 160),
 )
 SCALE_ROW = (4, 0)
 
@@ -54,7 +55,7 @@ def tile_moe_cap2_lin_bias_kernel(
         y = keep.tile([P, SLOTS + PAD], F32, align_bytes=64, name="y")
         nc.vector.memset(y[:, SLOTS:], 0.0)
 
-        for plane, scales, queue in ((s8, w8_scales, nc.gpsimd), (s4, w4_scales, nc.gpsimd)):
+        def load_scales(plane, scales, queue):
             view = plane[:].rearrange("p (e n) -> p e n", e=E)
             for q in range(4):
                 queue.dma_start(
@@ -62,19 +63,22 @@ def tile_moe_cap2_lin_bias_kernel(
                     in_=scales[:, 0, 4 * q : 4 * q + 4, :].rearrange("e q n -> q e n").bitcast(I32),
                 )
 
+
         raws = []
         for i, (a, t0, n, v) in enumerate(CHUNKS):
-            raw = keep.tile([P, PACK, n], F32, align_bytes=64, name="raw%d" % i)
+            raw = keep.tile([P, PACK, n], F32, align_bytes=64, name="raw%d" % i, tag="raw%d" % i)
             rows = xT[a * 512 : (a + 1) * 512, t0 : t0 + n]
             nc.sync.dma_start(out=raw[:], in_=rows.rearrange("(p j) t -> p j t", j=PACK))
             raws.append(raw)
-            if i == 1:
+            if i == 2:
                 nc.sync.dma_start(offs_sb[:], offs)
 
         w8 = keep.tile([P, E, 4 * N], U8, align_bytes=64, name="w8")
         nc.sync.dma_start(out=w8[:].bitcast(I32), in_=w8_words[:, 0].rearrange("e p n r -> p e (n r)").bitcast(I32))
         w4 = keep.tile([P, E, 2 * N], U8, align_bytes=64, name="w4")
         nc.sync.dma_start(out=w4[:].bitcast(I32), in_=w4_words[:, 0].rearrange("e p n -> p e n").bitcast(I32))
+        load_scales(s8, w8_scales, nc.sync)
+        load_scales(s4, w4_scales, nc.sync)
         bias = keep.tile([P, E], F32, name="bias")
         nc.sync.dma_start(out=bias[:], in_=b)
         nc.sync.dma_start(pos1_sb[:], pos1)
@@ -83,43 +87,47 @@ def tile_moe_cap2_lin_bias_kernel(
         nc.sync.dma_start(out=gates[:], in_=gate.rearrange("a p t -> p a t"))
 
         words = [keep.tile([P, T], U32, align_bytes=64, name="words%d" % a) for a in range(2)]
-        slot_words = [keep.tile([P, SLOTS], U32, align_bytes=64, name="slot_words%d" % a) for a in range(2)]
+        slot_words = [keep.tile([P, (SLOTS - 128, SLOTS)[a]], U32, align_bytes=64, name="slot_words%d" % a) for a in range(2)]
         slot_bytes = keep.tile([P, SLOTS], U8, align_bytes=64, name="slot_bytes")
 
-        grouped = [keep.tile([P, T, PACK], BF16, align_bytes=64, name="grouped%d" % a) for a in range(2)]
+        grouped = [keep.tile([P, n, PACK], BF16, align_bytes=64, name="grouped%d" % i) for i, (a, t0, n, v) in enumerate(CHUNKS)]
 
         def cast(i):
             a, t0, n, v = CHUNKS[i]
             for copy, c0, c1 in ((nc.vector.tensor_copy, 0, v), (nc.scalar.copy, v, n)):
                 if c0 < c1:
                     copy(
-                        grouped[a][:, t0 + c0 : t0 + c1, :].rearrange("p (c i) j -> p c j i", i=4),
+                        grouped[i][:, c0:c1, :].rearrange("p (c i) j -> p c j i", i=4),
                         raws[i][:, :, c0:c1].rearrange("p j (c i) -> p c j i", i=4),
                     )
 
-        def quantise(a, t0, n):
+        def quantise(i):
+            a, t0, n, v = CHUNKS[i]
             nc.vector.quantize_mx(
                 out=words[a][:, t0 : t0 + n].bitcast(E4M3X4),
                 scales=token_bytes[SCALE_ROW[a] : P, t0 : t0 + n],
-                in_=grouped[a][:, t0 : t0 + n, :].rearrange("p t j -> p (t j)"),
+                in_=grouped[i][:].rearrange("p t j -> p (t j)"),
             )
 
-        def gather(dst, src, s0, n):
-            nc.vector.tensor_copy(dst[:, s0 : s0 + n], src[:].indirect(offs_sb[:, s0 // 16 : (s0 + n) // 16]))
+        def gather(dst, src, s0, n, d0=0):
+            nc.vector.tensor_copy(dst[:, s0 - d0 : s0 - d0 + n], src[:].indirect(offs_sb[:, s0 // 16 : (s0 + n) // 16]))
 
         cast(0)
-        quantise(0, 0, 512)
+        quantise(0)
         cast(1)
-        quantise(0, 512, 256)
-        gather(slot_words[0], words[0], 0, 512)
+        quantise(1)
         cast(2)
-        gather(slot_words[0], words[0], 512, 384)
+        quantise(2)
+        gather(slot_words[0], words[0], 0, 512)
         cast(3)
-        quantise(1, 0, 256)
+        gather(slot_words[0], words[0], 512, 384)
+        quantise(3)
         cast(4)
-        quantise(1, 256, 256)
-        quantise(1, 512, 256)
-        gather(slot_words[0], words[0], 896, 128)
+        cast(5)
+        quantise(4)
+        quantise(5)
+        late_words = keep.tile([P, 128], U32, align_bytes=64, name="late_words", tag="raw5")
+        gather(late_words, words[0], 896, 128, 896)
 
         banks = [psum.tile([P, 128], F32, name="bank%d" % i) for i in range(SLOTS // 128)]
 
@@ -130,7 +138,7 @@ def tile_moe_cap2_lin_bias_kernel(
                 out=banks[i][:],
                 lhsT=(w8[:, e, :].bitcast(E4M3X4), w4[:, e, :].bitcast(E2M1X4))[a],
                 lhsT_scale=(s8, s4)[a][:, e * N : (e + 1) * N],
-                rhs=slot_words[a][:, s0 : s0 + 128].bitcast(E4M3X4),
+                rhs=(late_words[:] if (a, i) == (0, 7) else slot_words[a][:, s0 : s0 + 128]).bitcast(E4M3X4),
                 rhs_scale=slot_bytes[SCALE_ROW[a] : P, s0 : s0 + 128],
                 start=(a == 0),
                 stop=(a == 1),

@@ -31,6 +31,8 @@ CHUNKS = (
     (1, 512, 256, 160),
 )
 SCALE_ROW = (4, 0)
+BYTE_WINDOW = 1408
+WORD_WINDOW = 1216
 
 
 def tile_moe_cap2_lin_bias_kernel(
@@ -50,7 +52,7 @@ def tile_moe_cap2_lin_bias_kernel(
         s4 = keep.tile([P, E * N], U8, align_bytes=64, name="s4")
         nc.vector.memset(s8[:].bitcast(I32), 0)
         nc.vector.memset(s4[:].bitcast(I32), 0)
-        token_bytes = keep.tile([P, T], U8, align_bytes=64, name="token_bytes")
+        token_bytes = keep.tile([P, BYTE_WINDOW], U8, align_bytes=64, name="token_bytes")
         nc.vector.memset(token_bytes[:].bitcast(I32), 0)
         y = keep.tile([P, SLOTS + PAD], F32, align_bytes=64, name="y")
         nc.vector.memset(y[:, SLOTS:], 0.0)
@@ -86,7 +88,8 @@ def tile_moe_cap2_lin_bias_kernel(
         gates = keep.tile([P, 2, T], F32, align_bytes=64, name="gates")
         nc.sync.dma_start(out=gates[:], in_=gate.rearrange("a p t -> p a t"))
 
-        words = [keep.tile([P, T], U32, align_bytes=64, name="words%d" % a) for a in range(2)]
+        words = [keep.tile([P, (WORD_WINDOW, T)[a]], I32, align_bytes=64, name="words%d" % a) for a in range(2)]
+        nc.vector.memset(words[0][:, T:], 0)
         slot_words = [keep.tile([P, (SLOTS - 128, SLOTS)[a]], U32, align_bytes=64, name="slot_words%d" % a) for a in range(2)]
         slot_bytes = keep.tile([P, SLOTS], U8, align_bytes=64, name="slot_bytes")
 
@@ -110,7 +113,7 @@ def tile_moe_cap2_lin_bias_kernel(
             )
 
         def gather(dst, src, s0, n, d0=0):
-            nc.vector.tensor_copy(dst[:, s0 - d0 : s0 - d0 + n], src[:].indirect(offs_sb[:, s0 // 16 : (s0 + n) // 16]))
+            nc.vector.tensor_copy(dst[:, s0 - d0 : s0 - d0 + n], src.indirect(offs_sb[:, s0 // 16 : (s0 + n) // 16]))
 
         cast(0)
         quantise(0)
@@ -118,16 +121,15 @@ def tile_moe_cap2_lin_bias_kernel(
         quantise(1)
         cast(2)
         quantise(2)
-        gather(slot_words[0], words[0], 0, 512)
+        gather(slot_words[0], words[0][:].bitcast(U32), 0, 896)
         cast(3)
-        gather(slot_words[0], words[0], 512, 384)
         quantise(3)
         cast(4)
         cast(5)
         quantise(4)
         quantise(5)
         late_words = keep.tile([P, 128], U32, align_bytes=64, name="late_words", tag="raw5")
-        gather(late_words, words[0], 896, 128, 896)
+        gather(late_words, words[0][:, :T].bitcast(U32), 896, 128, 896)
 
         banks = [psum.tile([P, 128], F32, name="bank%d" % i) for i in range(SLOTS // 128)]
 
@@ -144,13 +146,12 @@ def tile_moe_cap2_lin_bias_kernel(
                 stop=(a == 1),
             )
 
-        for s0 in (0, 512):
-            gather(slot_bytes, token_bytes, s0, 512)
-            for i in range(s0 // 128, s0 // 128 + 4):
-                multiply(0, i)
+        gather(slot_bytes, token_bytes[:], 0, SLOTS)
+        for i in range(SLOTS // 128):
+            multiply(0, i)
 
-        for s0, n in ((0, 512), (512, 384), (896, 128)):
-            gather(slot_words[1], words[1], s0, n)
+        for s0, n in ((0, 512), (512, 256), (768, 128), (896, 128)):
+            gather(slot_words[1], words[1][:].bitcast(U32), s0, n)
             for i in range(s0 // 128, (s0 + n) // 128):
                 multiply(1, i)
                 e = i // 2
@@ -173,10 +174,10 @@ def tile_moe_cap2_lin_bias_kernel(
             nc.vector.tensor_tensor(result[:, cols], first[:, cols], second[:, cols], ADD)
             nc.sync.dma_start(out=out[:, cols], in_=result[:, cols])
 
-        weigh(first, 0, pos1_sb, 0, 512)
-        weigh(second, 1, pos2_sb, 0, 512)
-        weigh(first, 0, pos1_sb, 512, 256)
-        finish(0, 256)
-        weigh(second, 1, pos2_sb, 512, 256)
-        finish(256, 256)
-        finish(512, 256)
+        weigh(first, 0, pos1_sb, 0, T)
+        weigh(second, 1, pos2_sb, 0, 384)
+        weigh(second, 1, pos2_sb, 384, 256)
+        finish(0, 384)
+        weigh(second, 1, pos2_sb, 640, 128)
+        finish(384, 256)
+        finish(640, 128)

@@ -22,13 +22,14 @@ MULT = mybir.AluOpType.mult
 ADD = mybir.AluOpType.add
 IDENTITY = mybir.ActivationFunctionType.Identity
 
+LOADS = ((0, 0, 512), (0, 512, 256), (1, 0, 512), (1, 512, 256))
 CHUNKS = (
     (0, 0, 256, 160),
-    (0, 256, 256, 160),
-    (0, 512, 256, 160),
-    (1, 0, 256, 0),
-    (1, 256, 256, 0),
-    (1, 512, 256, 160),
+    (0, 256, 256, 128),
+    (1, 0, 256, 160),
+    (2, 0, 256, 0),
+    (2, 256, 256, 128),
+    (3, 0, 256, 128),
 )
 SCALE_ROW = (4, 0)
 BYTE_WINDOW = 1408
@@ -67,12 +68,12 @@ def tile_moe_cap2_lin_bias_kernel(
 
 
         raws = []
-        for i, (a, t0, n, v) in enumerate(CHUNKS):
+        for i, (a, t0, n) in enumerate(LOADS):
             raw = keep.tile([P, PACK, n], F32, align_bytes=64, name="raw%d" % i, tag="raw%d" % i)
             rows = xT[a * 512 : (a + 1) * 512, t0 : t0 + n]
             nc.sync.dma_start(out=raw[:], in_=rows.rearrange("(p j) t -> p j t", j=PACK))
             raws.append(raw)
-            if i == 2:
+            if i == 1:
                 nc.sync.dma_start(offs_sb[:], offs)
 
         w8 = keep.tile([P, E, 4 * N], U8, align_bytes=64, name="w8")
@@ -96,16 +97,17 @@ def tile_moe_cap2_lin_bias_kernel(
         grouped = [keep.tile([P, n, PACK], BF16, align_bytes=64, name="grouped%d" % i) for i, (a, t0, n, v) in enumerate(CHUNKS)]
 
         def cast(i):
-            a, t0, n, v = CHUNKS[i]
+            load, t0, n, v = CHUNKS[i]
             for copy, c0, c1 in ((nc.vector.tensor_copy, 0, v), (nc.scalar.copy, v, n)):
                 if c0 < c1:
                     copy(
                         grouped[i][:, c0:c1, :].rearrange("p (c i) j -> p c j i", i=4),
-                        raws[i][:, :, c0:c1].rearrange("p j (c i) -> p c j i", i=4),
+                        raws[load][:, :, t0 + c0 : t0 + c1].rearrange("p j (c i) -> p c j i", i=4),
                     )
 
         def quantise(i):
-            a, t0, n, v = CHUNKS[i]
+            load, t0, n, v = CHUNKS[i]
+            a, t0 = LOADS[load][0], LOADS[load][1] + t0
             nc.vector.quantize_mx(
                 out=words[a][:, t0 : t0 + n].bitcast(E4M3X4),
                 scales=token_bytes[SCALE_ROW[a] : P, t0 : t0 + n],
@@ -116,19 +118,19 @@ def tile_moe_cap2_lin_bias_kernel(
             nc.vector.tensor_copy(dst[:, s0 - d0 : s0 - d0 + n], src.indirect(offs_sb[:, s0 // 16 : (s0 + n) // 16]))
 
         cast(0)
-        quantise(0)
         cast(1)
+        quantise(0)
         quantise(1)
         cast(2)
         quantise(2)
         gather(slot_words[0], words[0][:].bitcast(U32), 0, 896)
         cast(3)
-        quantise(3)
         cast(4)
+        quantise(3)
         cast(5)
         quantise(4)
         quantise(5)
-        late_words = keep.tile([P, 128], U32, align_bytes=64, name="late_words", tag="raw5")
+        late_words = keep.tile([P, 128], U32, align_bytes=64, name="late_words", tag="raw3")
         gather(late_words, words[0][:, :T].bitcast(U32), 896, 128, 896)
 
         banks = [psum.tile([P, 128], F32, name="bank%d" % i) for i in range(SLOTS // 128)]

@@ -22,17 +22,17 @@ MULT = mybir.AluOpType.mult
 ADD = mybir.AluOpType.add
 IDENTITY = mybir.ActivationFunctionType.Identity
 
-LOADS = ((0, 0, 512), (0, 512, 256), (1, 0, 512), (1, 512, 256))
+LOADS = ((0, 0, 512), (0, 512, 256), (1, 0, 256), (1, 256, 256), (1, 512, 256))
 CHUNKS = (
-    (0, 0, 256, 160),
+    (0, 0, 256, 192),
     (0, 256, 256, 128),
     (1, 0, 256, 160),
     (2, 0, 256, 0),
-    (2, 256, 256, 128),
-    (3, 0, 256, 128),
+    (3, 0, 256, 0),
+    (4, 0, 256, 160),
 )
 SCALE_ROW = (4, 0)
-BYTE_WINDOW = 1408
+BYTE_WINDOW = T
 WORD_WINDOW = 1216
 
 
@@ -87,7 +87,8 @@ def tile_moe_cap2_lin_bias_kernel(
         nc.sync.dma_start(pos1_sb[:], pos1)
         nc.sync.dma_start(pos2_sb[:], pos2)
         gates = keep.tile([P, 2, T], F32, align_bytes=64, name="gates")
-        nc.sync.dma_start(out=gates[:], in_=gate.rearrange("a p t -> p a t"))
+        for which in range(2):
+            nc.sync.dma_start(out=gates[:, which, :], in_=gate[which])
 
         words = [keep.tile([P, (WORD_WINDOW, T)[a]], I32, align_bytes=64, name="words%d" % a) for a in range(2)]
         nc.vector.memset(words[0][:, T:], 0)
@@ -120,17 +121,17 @@ def tile_moe_cap2_lin_bias_kernel(
         cast(0)
         cast(1)
         quantise(0)
-        quantise(1)
         cast(2)
+        quantise(1)
         quantise(2)
         gather(slot_words[0], words[0][:].bitcast(U32), 0, 896)
         cast(3)
-        cast(4)
         quantise(3)
+        cast(4)
         cast(5)
         quantise(4)
         quantise(5)
-        late_words = keep.tile([P, 128], U32, align_bytes=64, name="late_words", tag="raw3")
+        late_words = keep.tile([P, 128], U32, align_bytes=64, name="late_words", tag="raw4")
         gather(late_words, words[0][:, :T].bitcast(U32), 896, 128, 896)
 
         banks = [psum.tile([P, 128], F32, name="bank%d" % i) for i in range(SLOTS // 128)]
@@ -148,11 +149,12 @@ def tile_moe_cap2_lin_bias_kernel(
                 stop=(a == 1),
             )
 
-        gather(slot_bytes, token_bytes[:], 0, SLOTS)
-        for i in range(SLOTS // 128):
-            multiply(0, i)
+        for s0 in (0, 512):
+            gather(slot_bytes, token_bytes[:], s0, 512)
+            for i in range(s0 // 128, s0 // 128 + 4):
+                multiply(0, i)
 
-        for s0, n in ((0, 512), (512, 256), (768, 128), (896, 128)):
+        for s0, n in ((0, 256), (256, 256), (512, 256), (768, 128), (896, 128)):
             gather(slot_words[1], words[1][:].bitcast(U32), s0, n)
             for i in range(s0 // 128, (s0 + n) // 128):
                 multiply(1, i)

@@ -21,6 +21,7 @@ E2M1X4 = mybir.dt.float4_e2m1fn_x4
 MULT = mybir.AluOpType.mult
 ADD = mybir.AluOpType.add
 IDENTITY = mybir.ActivationFunctionType.Identity
+COPY = mybir.ActivationFunctionType.Copy
 
 LOADS = ((0, 0, 512), (0, 512, 256), (1, 0, 256), (1, 256, 256), (1, 512, 256))
 CHUNKS = (
@@ -86,9 +87,9 @@ def tile_moe_cap2_lin_bias_kernel(
         nc.sync.dma_start(out=bias[:], in_=b)
         nc.sync.dma_start(pos1_sb[:], pos1)
         nc.sync.dma_start(pos2_sb[:], pos2)
-        gates = keep.tile([P, 2, T], F32, align_bytes=64, name="gates")
+        gates = [keep.tile([P, T], F32, align_bytes=64, name="gates%d" % which) for which in range(2)]
         for which in range(2):
-            nc.sync.dma_start(out=gates[:, which, :], in_=gate[which])
+            nc.sync.dma_start(out=gates[which][:], in_=gate[which])
 
         words = [keep.tile([P, (WORD_WINDOW, T)[a]], I32, align_bytes=64, name="words%d" % a) for a in range(2)]
         nc.vector.memset(words[0][:, T:], 0)
@@ -165,23 +166,40 @@ def tile_moe_cap2_lin_bias_kernel(
                 else:
                     nc.vector.tensor_scalar(y[:, cols], banks[i][:], bias[:, e : e + 1], None, ADD)
 
-        first = keep.tile([P, T], F32, align_bytes=64, name="first")
-        second = keep.tile([P, T], F32, align_bytes=64, name="second")
+        weighted = [keep.tile([P, T], F32, align_bytes=64, name="weighted%d" % which) for which in range(2)]
         result = keep.tile([P, T], F32, align_bytes=64, name="result")
+        choices = (pos1_sb, pos2_sb)
+        fetched = {}
 
-        def weigh(target, which, entries_sb, t0, n):
+        def slots_of(which, t0, n):
+            return y[:].indirect(choices[which][:, t0 // 16 : (t0 + n) // 16])
+
+        def fetch(which, t0, n):
+            fetched[which, t0] = keep.tile([P, n], F32, align_bytes=64, name="fetched%d_%d" % (which, t0))
+            nc.scalar.activation(fetched[which, t0][:], slots_of(which, t0, n), COPY)
+
+        def fetch_and_weigh(which, t0, n):
             cols = slice(t0, t0 + n)
-            nc.vector.tensor_tensor(target[:, cols], y[:].indirect(entries_sb[:, t0 // 16 : (t0 + n) // 16]), gates[:, which, cols], MULT)
+            nc.vector.tensor_tensor(weighted[which][:, cols], slots_of(which, t0, n), gates[which][:, cols], MULT)
+
+        def weigh(which, t0, n):
+            cols = slice(t0, t0 + n)
+            nc.vector.tensor_tensor(weighted[which][:, cols], fetched[which, t0][:], gates[which][:, cols], MULT)
 
         def finish(t0, n):
             cols = slice(t0, t0 + n)
-            nc.vector.tensor_tensor(result[:, cols], first[:, cols], second[:, cols], ADD)
+            nc.vector.tensor_tensor(result[:, cols], weighted[0][:, cols], weighted[1][:, cols], ADD)
             nc.sync.dma_start(out=out[:, cols], in_=result[:, cols])
 
-        weigh(first, 0, pos1_sb, 0, T)
-        weigh(second, 1, pos2_sb, 0, 384)
-        weigh(second, 1, pos2_sb, 384, 256)
-        finish(0, 384)
-        weigh(second, 1, pos2_sb, 640, 128)
-        finish(384, 256)
-        finish(640, 128)
+        fetch(1, 0, 256)
+        fetch_and_weigh(0, 0, 512)
+        fetch(1, 256, 256)
+        fetch(0, 512, 256)
+        fetch(1, 512, 256)
+        weigh(1, 0, 256)
+        weigh(1, 256, 256)
+        finish(0, 256)
+        weigh(0, 512, 256)
+        weigh(1, 512, 256)
+        finish(256, 256)
+        finish(512, 256)

@@ -166,40 +166,42 @@ def tile_moe_cap2_lin_bias_kernel(
                 else:
                     nc.vector.tensor_scalar(y[:, cols], banks[i][:], bias[:, e : e + 1], None, ADD)
 
-        weighted = [keep.tile([P, T], F32, align_bytes=64, name="weighted%d" % which) for which in range(2)]
-        result = keep.tile([P, T], F32, align_bytes=64, name="result")
         choices = (pos1_sb, pos2_sb)
-        fetched = {}
+
+        def block(name, n=256):
+            return keep.tile([P, n], F32, align_bytes=64, name=name)
 
         def slots_of(which, t0, n):
             return y[:].indirect(choices[which][:, t0 // 16 : (t0 + n) // 16])
 
-        def fetch(which, t0, n):
-            fetched[which, t0] = keep.tile([P, n], F32, align_bytes=64, name="fetched%d_%d" % (which, t0))
-            nc.scalar.activation(fetched[which, t0][:], slots_of(which, t0, n), COPY)
+        def fetch(target, which, t0, n):
+            nc.scalar.activation(target, slots_of(which, t0, n), COPY)
 
-        def fetch_and_weigh(which, t0, n):
-            cols = slice(t0, t0 + n)
-            nc.vector.tensor_tensor(weighted[which][:, cols], slots_of(which, t0, n), gates[which][:, cols], MULT)
+        def weigh(target, source, which, t0, n):
+            nc.vector.tensor_tensor(target, source, gates[which][:, t0 : t0 + n], MULT)
 
-        def weigh(which, t0, n):
-            cols = slice(t0, t0 + n)
-            nc.vector.tensor_tensor(weighted[which][:, cols], fetched[which, t0][:], gates[which][:, cols], MULT)
+        def add(target, first, second):
+            nc.vector.tensor_tensor(target, first, second, ADD)
 
-        def finish(t0, n):
-            cols = slice(t0, t0 + n)
-            nc.vector.tensor_tensor(result[:, cols], weighted[0][:, cols], weighted[1][:, cols], ADD)
-            nc.sync.dma_start(out=out[:, cols], in_=result[:, cols])
-
-        fetch(1, 0, 256)
-        fetch_and_weigh(0, 0, 512)
-        fetch(1, 256, 256)
-        fetch(0, 512, 256)
-        fetch(1, 512, 256)
-        weigh(1, 0, 256)
-        weigh(1, 256, 256)
-        finish(0, 256)
-        weigh(0, 512, 256)
-        weigh(1, 512, 256)
-        finish(256, 256)
-        finish(512, 256)
+        direct = block("direct", 512)
+        got = [block("got%d" % i) for i in range(4)]
+        made = [block("made%d" % i) for i in range(2)]
+        result = block("result", T)
+        fetch(got[0][:], 1, 0, 256)
+        weigh(direct[:], slots_of(0, 0, 512), 0, 0, 512)
+        fetch(got[1][:], 1, 256, 256)
+        fetch(got[2][:], 0, 512, 256)
+        fetch(got[3][:, :128], 1, 512, 128)
+        fetch(got[3][:, 128:], 1, 640, 128)
+        weigh(made[0][:], got[0][:], 1, 0, 256)
+        weigh(made[1][:], got[1][:], 1, 256, 256)
+        add(result[:, 0:256], direct[:, :256], made[0][:])
+        nc.sync.dma_start(out=out[:, 0:256], in_=result[:, 0:256])
+        add(result[:, 256:512], direct[:, 256:], made[1][:])
+        nc.sync.dma_start(out=out[:, 256:512], in_=result[:, 256:512])
+        weigh(made[0][:], got[2][:], 0, 512, 256)
+        weigh(made[1][:, :128], got[3][:, :128], 1, 512, 128)
+        weigh(made[1][:, 128:], got[3][:, 128:], 1, 640, 128)
+        add(result[:, 512:640], made[0][:, :128], made[1][:, :128])
+        add(result[:, 640:768], made[0][:, 128:], made[1][:, 128:])
+        nc.sync.dma_start(out=out[:, 512:768], in_=result[:, 512:768])

@@ -88,7 +88,7 @@ def tile_moe_cap2_lin_bias_kernel(
         nc.sync.dma_start(pos1_sb[:], pos1)
         nc.sync.dma_start(pos2_sb[:], pos2)
         gates = [keep.tile([P, T], F32, align_bytes=64, name="gates%d" % which) for which in range(2)]
-        for which in range(2):
+        for which in (1, 0):
             nc.sync.dma_start(out=gates[which][:], in_=gate[which])
 
         words = [keep.tile([P, (WORD_WINDOW, T)[a]], I32, align_bytes=64, name="words%d" % a) for a in range(2)]
@@ -183,25 +183,23 @@ def tile_moe_cap2_lin_bias_kernel(
         def add(target, first, second):
             nc.vector.tensor_tensor(target, first, second, ADD)
 
-        direct = block("direct", 512)
-        got = [block("got%d" % i) for i in range(4)]
+        direct = block("direct", T)
+        got = [block("got%d" % i, n) for i, n in enumerate((256, 256, 128, 128))]
         made = [block("made%d" % i) for i in range(2)]
         result = block("result", T)
-        fetch(got[0][:], 1, 0, 256)
-        weigh(direct[:], slots_of(0, 0, 512), 0, 0, 512)
-        fetch(got[1][:], 1, 256, 256)
-        fetch(got[2][:], 0, 512, 256)
-        fetch(got[3][:, :128], 1, 512, 128)
-        fetch(got[3][:, 128:], 1, 640, 128)
-        weigh(made[0][:], got[0][:], 1, 0, 256)
-        weigh(made[1][:], got[1][:], 1, 256, 256)
+        fetch(got[0][:], 0, 0, 256)
+        weigh(direct[:], slots_of(1, 0, T), 1, 0, T)
+        fetch(got[1][:], 0, 256, 256)
+        fetch(got[2][:], 0, 512, 128)
+        fetch(got[3][:], 0, 640, 128)
+        weigh(made[0][:], got[0][:], 0, 0, 256)
+        weigh(made[1][:], got[1][:], 0, 256, 256)
         add(result[:, 0:256], direct[:, :256], made[0][:])
         nc.sync.dma_start(out=out[:, 0:256], in_=result[:, 0:256])
-        add(result[:, 256:512], direct[:, 256:], made[1][:])
+        add(result[:, 256:512], direct[:, 256:512], made[1][:])
         nc.sync.dma_start(out=out[:, 256:512], in_=result[:, 256:512])
-        weigh(made[0][:], got[2][:], 0, 512, 256)
-        weigh(made[1][:, :128], got[3][:, :128], 1, 512, 128)
-        weigh(made[1][:, 128:], got[3][:, 128:], 1, 640, 128)
-        add(result[:, 512:640], made[0][:, :128], made[1][:, :128])
-        add(result[:, 640:768], made[0][:, 128:], made[1][:, 128:])
+        weigh(made[0][:, :128], got[2][:], 0, 512, 128)
+        weigh(made[1][:, :128], got[3][:], 0, 640, 128)
+        add(result[:, 512:640], direct[:, 512:640], made[0][:, :128])
+        add(result[:, 640:768], direct[:, 640:768], made[1][:, :128])
         nc.sync.dma_start(out=out[:, 512:768], in_=result[:, 512:768])

@@ -32,6 +32,7 @@ CHUNKS = (
     (3, 0, 256, 0),
     (4, 0, 256, 160),
 )
+GROUPS = ((0, 256), (256, 256), (512, 256), (768, 128), (896, 128))
 SCALE_ROW = (4, 0)
 BYTE_WINDOW = T
 WORD_WINDOW = 1216
@@ -135,36 +136,36 @@ def tile_moe_cap2_lin_bias_kernel(
         late_words = keep.tile([P, 128], U32, align_bytes=64, name="late_words", tag="raw4")
         gather(late_words, words[0][:, :T].bitcast(U32), 896, 128, 896)
 
-        banks = [psum.tile([P, 128], F32, name="bank%d" % i) for i in range(SLOTS // 128)]
+        banks = [psum.tile([P, n], F32, name="bank%d" % g) for g, (s0, n) in enumerate(GROUPS)]
 
-        def multiply(a, i):
-            s0 = 128 * i
+        def multiply(a, g):
+            s0, n = GROUPS[g]
             e = s0 // C
             nc.tensor.matmul_mx(
-                out=banks[i][:],
+                out=banks[g][:],
                 lhsT=(w8[:, e, :].bitcast(E4M3X4), w4[:, e, :].bitcast(E2M1X4))[a],
                 lhsT_scale=(s8, s4)[a][:, e * N : (e + 1) * N],
-                rhs=(late_words[:] if (a, i) == (0, 7) else slot_words[a][:, s0 : s0 + 128]).bitcast(E4M3X4),
-                rhs_scale=slot_bytes[SCALE_ROW[a] : P, s0 : s0 + 128],
+                rhs=(late_words[:] if (a, s0) == (0, 896) else slot_words[a][:, s0 : s0 + n]).bitcast(E4M3X4),
+                rhs_scale=slot_bytes[SCALE_ROW[a] : P, s0 : s0 + n],
                 start=(a == 0),
                 stop=(a == 1),
             )
 
-        for s0 in (0, 512):
-            gather(slot_bytes, token_bytes[:], s0, 512)
-            for i in range(s0 // 128, s0 // 128 + 4):
-                multiply(0, i)
+        for half in (0, 512):
+            gather(slot_bytes, token_bytes[:], half, 512)
+            for g, (s0, n) in enumerate(GROUPS):
+                if half <= s0 < half + 512:
+                    multiply(0, g)
 
-        for s0, n in ((0, 256), (256, 256), (512, 256), (768, 128), (896, 128)):
+        for g, (s0, n) in enumerate(GROUPS):
             gather(slot_words[1], words[1][:].bitcast(U32), s0, n)
-            for i in range(s0 // 128, (s0 + n) // 128):
-                multiply(1, i)
-                e = i // 2
-                cols = slice(128 * i, 128 * i + 128)
-                if i != 6:
-                    nc.scalar.activation(y[:, cols], banks[i][:], IDENTITY, bias=bias[:, e : e + 1], scale=1.0)
-                else:
-                    nc.vector.tensor_scalar(y[:, cols], banks[i][:], bias[:, e : e + 1], None, ADD)
+            multiply(1, g)
+            e = s0 // C
+            cols = slice(s0, s0 + n)
+            if g != 3:
+                nc.scalar.activation(y[:, cols], banks[g][:], IDENTITY, bias=bias[:, e : e + 1], scale=1.0)
+            else:
+                nc.vector.tensor_scalar(y[:, cols], banks[g][:], bias[:, e : e + 1], None, ADD)
 
         choices = (pos1_sb, pos2_sb)
 

@@ -185,22 +185,23 @@ def tile_moe_cap2_lin_bias_kernel(
             nc.vector.tensor_tensor(target, first, second, ADD)
 
         direct = block("direct", T)
-        got = [block("got%d" % i, n) for i, n in enumerate((256, 256, 128, 128))]
-        made = [block("made%d" % i) for i in range(2)]
+        got = [block("got%d" % i, n) for i, n in enumerate((256, 256, 128, 64))]
+        made = [block("made%d" % i, n) for i, n in enumerate((320, 256, 128))]
         result = block("result", T)
         fetch(got[0][:], 0, 0, 256)
         weigh(direct[:], slots_of(1, 0, T), 1, 0, T)
+        weigh(made[0][:, :64], slots_of(0, 640, 64), 0, 640, 64)
         fetch(got[1][:], 0, 256, 256)
         fetch(got[2][:], 0, 512, 128)
-        fetch(got[3][:], 0, 640, 128)
-        weigh(made[0][:], got[0][:], 0, 0, 256)
+        fetch(got[3][:], 0, 704, 64)
+        weigh(made[0][:, 64:], got[0][:], 0, 0, 256)
         weigh(made[1][:], got[1][:], 0, 256, 256)
-        add(result[:, 0:256], direct[:, :256], made[0][:])
+        add(result[:, 0:256], direct[:, :256], made[0][:, 64:])
         nc.sync.dma_start(out=out[:, 0:256], in_=result[:, 0:256])
+        weigh(made[2][:], got[2][:], 0, 512, 128)
+        weigh(made[0][:, 64:128], got[3][:], 0, 704, 64)
         add(result[:, 256:512], direct[:, 256:512], made[1][:])
         nc.sync.dma_start(out=out[:, 256:512], in_=result[:, 256:512])
-        weigh(made[0][:, :128], got[2][:], 0, 512, 128)
-        weigh(made[1][:, :128], got[3][:], 0, 640, 128)
-        add(result[:, 512:640], direct[:, 512:640], made[0][:, :128])
-        add(result[:, 640:768], direct[:, 640:768], made[1][:, :128])
+        add(result[:, 512:640], direct[:, 512:640], made[2][:])
+        add(result[:, 640:768], direct[:, 640:768], made[0][:, :128])
         nc.sync.dma_start(out=out[:, 512:768], in_=result[:, 512:768])

@@ -104,8 +104,8 @@ def tile_moe_cap2_lin_bias_kernel(
             for copy, c0, c1 in ((nc.vector.tensor_copy, 0, v), (nc.scalar.copy, v, n)):
                 if c0 < c1:
                     copy(
-                        grouped[i][:, c0:c1, :].rearrange("p (c i) j -> p c j i", i=4),
-                        raws[load][:, :, t0 + c0 : t0 + c1].rearrange("p j (c i) -> p c j i", i=4),
+                        grouped[i][:, c0:c1, :].rearrange("p (c i) j -> p c j i", i=2),
+                        raws[load][:, :, t0 + c0 : t0 + c1].rearrange("p j (c i) -> p c j i", i=2),
                     )
 
         def quantise(i):

@@ -25,8 +25,8 @@ COPY = mybir.ActivationFunctionType.Copy
 
 LOADS = ((0, 0, 512), (0, 512, 256), (1, 0, 256), (1, 256, 256), (1, 512, 256))
 CHUNKS = (
-    (0, 0, 256, 192),
-    (0, 256, 256, 128),
+    (0, 0, 256, 256),
+    (0, 256, 256, 64),
     (1, 0, 256, 160),
     (2, 0, 256, 0),
     (3, 0, 256, 0),
@@ -54,7 +54,7 @@ def tile_moe_cap2_lin_bias_kernel(
         s8 = keep.tile([P, E * N], U8, align_bytes=64, name="s8")
         s4 = keep.tile([P, E * N], U8, align_bytes=64, name="s4")
         nc.vector.memset(s8[:].bitcast(I32), 0)
-        nc.vector.memset(s4[:].bitcast(I32), 0)
+        nc.gpsimd.memset(s4[:].bitcast(I32), 0)
         token_bytes = keep.tile([P, BYTE_WINDOW], U8, align_bytes=64, name="token_bytes")
         nc.vector.memset(token_bytes[:].bitcast(I32), 0)
         y = keep.tile([P, SLOTS + PAD], F32, align_bytes=64, name="y")
@@ -162,10 +162,7 @@ def tile_moe_cap2_lin_bias_kernel(
             multiply(1, g)
             e = s0 // C
             cols = slice(s0, s0 + n)
-            if g != 3:
-                nc.scalar.activation(y[:, cols], banks[g][:], IDENTITY, bias=bias[:, e : e + 1], scale=1.0)
-            else:
-                nc.vector.tensor_scalar(y[:, cols], banks[g][:], bias[:, e : e + 1], None, ADD)
+            nc.scalar.activation(y[:, cols], banks[g][:], IDENTITY, bias=bias[:, e : e + 1], scale=1.0)
 
         choices = (pos1_sb, pos2_sb)
 

@@ -36,6 +36,7 @@ GROUPS = ((0, 256), (256, 256), (512, 256), (768, 128), (896, 128))
 SCALE_ROW = (4, 0)
 BYTE_WINDOW = T
 WORD_WINDOW = 1216
+FIRST_BYTE = 128
 
 
 def tile_moe_cap2_lin_bias_kernel(
@@ -47,17 +48,27 @@ def tile_moe_cap2_lin_bias_kernel(
         keep = ctx.enter_context(tc.tile_pool(name="keep", bufs=1))
         psum = ctx.enter_context(tc.psum_pool(name="psum", bufs=1))
 
+        free = {"next": FIRST_BYTE}
+
+        def place(shape, dtype, size, name, align=64):
+            count = 1
+            for n in shape[1:]:
+                count = count * n
+            at = free["next"]
+            free.update({"next": at + -(-count * size // 64) * 64})
+            return keep.tile(shape, dtype, align_bytes=align, name=name, offset=at)
+
         offs_sb = lists.tile([P, SLOTS // 16], U16, name="offs_sb")
         pos1_sb = lists.tile([P, T // 16], U16, name="pos1_sb")
         pos2_sb = lists.tile([P, T // 16], U16, name="pos2_sb")
 
-        s8 = keep.tile([P, E * N], U8, align_bytes=64, name="s8")
-        s4 = keep.tile([P, E * N], U8, align_bytes=64, name="s4")
+        s8 = place([P, E * N], U8, 1, "s8")
+        s4 = place([P, E * N], U8, 1, "s4")
         nc.vector.memset(s8[:].bitcast(I32), 0)
         nc.gpsimd.memset(s4[:].bitcast(I32), 0)
-        token_bytes = keep.tile([P, BYTE_WINDOW], U8, align_bytes=64, name="token_bytes")
+        token_bytes = place([P, BYTE_WINDOW], U8, 1, "token_bytes")
         nc.vector.memset(token_bytes[:].bitcast(I32), 0)
-        y = keep.tile([P, SLOTS + PAD], F32, align_bytes=64, name="y")
+        y = place([P, SLOTS + PAD], F32, 4, "y")
         nc.vector.memset(y[:, SLOTS:], 0.0)
 
         def load_scales(plane, scales, queue):
@@ -71,33 +82,34 @@ def tile_moe_cap2_lin_bias_kernel(
 
         raws = []
         for i, (a, t0, n) in enumerate(LOADS):
-            raw = keep.tile([P, PACK, n], F32, align_bytes=64, name="raw%d" % i, tag="raw%d" % i)
+            last_raw = free["next"]
+            raw = place([P, PACK, n], F32, 4, "raw%d" % i, 256)
             rows = xT[a * 512 : (a + 1) * 512, t0 : t0 + n]
             nc.sync.dma_start(out=raw[:], in_=rows.rearrange("(p j) t -> p j t", j=PACK))
             raws.append(raw)
             if i == 1:
                 nc.sync.dma_start(offs_sb[:], offs)
 
-        w8 = keep.tile([P, E, 4 * N], U8, align_bytes=64, name="w8")
+        w8 = place([P, E, 4 * N], U8, 1, "w8")
         nc.sync.dma_start(out=w8[:].bitcast(I32), in_=w8_words[:, 0].rearrange("e p n r -> p e (n r)").bitcast(I32))
-        w4 = keep.tile([P, E, 2 * N], U8, align_bytes=64, name="w4")
+        w4 = place([P, E, 2 * N], U8, 1, "w4")
         nc.sync.dma_start(out=w4[:].bitcast(I32), in_=w4_words[:, 0].rearrange("e p n -> p e n").bitcast(I32))
         load_scales(s8, w8_scales, nc.sync)
         load_scales(s4, w4_scales, nc.sync)
-        bias = keep.tile([P, E], F32, name="bias")
+        bias = place([P, E], F32, 4, "bias")
         nc.sync.dma_start(out=bias[:], in_=b)
         nc.sync.dma_start(pos1_sb[:], pos1)
         nc.sync.dma_start(pos2_sb[:], pos2)
-        gates = [keep.tile([P, T], F32, align_bytes=64, name="gates%d" % which) for which in range(2)]
+        gates = [place([P, T], F32, 4, "gates%d" % which) for which in range(2)]
         for which in (1, 0):
             nc.sync.dma_start(out=gates[which][:], in_=gate[which])
 
-        words = [keep.tile([P, (WORD_WINDOW, T)[a]], I32, align_bytes=64, name="words%d" % a) for a in range(2)]
+        words = [place([P, (WORD_WINDOW, T)[a]], I32, 4, "words%d" % a) for a in range(2)]
         nc.vector.memset(words[0][:, T:], 0)
-        slot_words = [keep.tile([P, (SLOTS - 128, SLOTS)[a]], U32, align_bytes=64, name="slot_words%d" % a) for a in range(2)]
-        slot_bytes = keep.tile([P, SLOTS], U8, align_bytes=64, name="slot_bytes")
+        slot_words = [place([P, (SLOTS - 128, SLOTS)[a]], U32, 4, "slot_words%d" % a) for a in range(2)]
+        slot_bytes = place([P, SLOTS], U8, 1, "slot_bytes")
 
-        grouped = [keep.tile([P, n, PACK], BF16, align_bytes=64, name="grouped%d" % i) for i, (a, t0, n, v) in enumerate(CHUNKS)]
+        grouped = [place([P, n, PACK], BF16, 2, "grouped%d" % i) for i, (a, t0, n, v) in enumerate(CHUNKS)]
 
         def cast(i):
             load, t0, n, v = CHUNKS[i]
@@ -133,7 +145,7 @@ def tile_moe_cap2_lin_bias_kernel(
         cast(5)
         quantise(4)
         quantise(5)
-        late_words = keep.tile([P, 128], U32, align_bytes=64, name="late_words", tag="raw4")
+        late_words = keep.tile([P, 128], U32, align_bytes=64, name="late_words", offset=last_raw)
         gather(late_words, words[0][:, :T].bitcast(U32), 896, 128, 896)
 
         banks = [psum.tile([P, n], F32, name="bank%d" % g) for g, (s0, n) in enumerate(GROUPS)]
@@ -166,8 +178,8 @@ def tile_moe_cap2_lin_bias_kernel(
 
         choices = (pos1_sb, pos2_sb)
 
-        def block(name, n=256):
-            return keep.tile([P, n], F32, align_bytes=64, name=name)
+        def block(name, n):
+            return place([P, n], F32, 4, name)
 
         def slots_of(which, t0, n):
             return y[:].indirect(choices[which][:, t0 // 16 : (t0 + n) // 16])

@@ -27,10 +27,10 @@ LOADS = ((0, 0, 512), (0, 512, 256), (1, 0, 256), (1, 256, 256), (1, 512, 256))
 CHUNKS = (
     (0, 0, 256, 256),
     (0, 256, 256, 64),
-    (1, 0, 256, 160),
+    (1, 0, 256, 144),
     (2, 0, 256, 0),
     (3, 0, 256, 0),
-    (4, 0, 256, 160),
+    (4, 0, 256, 128),
 )
 GROUPS = ((0, 256), (256, 256), (512, 256), (768, 128), (896, 128))
 SCALE_ROW = (4, 0)
@@ -58,7 +58,7 @@ def tile_moe_cap2_lin_bias_kernel(
             free.update({"next": at + -(-count * size // 64) * 64})
             return keep.tile(shape, dtype, align_bytes=align, name=name, offset=at)
 
-        offs_sb = lists.tile([P, SLOTS // 16], U16, name="offs_sb")
+        offs_sb = lists.tile([P, SLOTS // 16], U16, align_bytes=256, name="offs_sb")
         pos1_sb = lists.tile([P, T // 16], U16, name="pos1_sb")
         pos2_sb = lists.tile([P, T // 16], U16, name="pos2_sb")
 
@@ -96,7 +96,7 @@ def tile_moe_cap2_lin_bias_kernel(
         nc.sync.dma_start(out=w4[:].bitcast(I32), in_=w4_words[:, 0].rearrange("e p n -> p e n").bitcast(I32))
         load_scales(s8, w8_scales, nc.sync)
         load_scales(s4, w4_scales, nc.sync)
-        bias = place([P, E], F32, 4, "bias")
+        bias = keep.tile([P, E], F32, align_bytes=64, name="bias", offset=0)
         nc.sync.dma_start(out=bias[:], in_=b)
         nc.sync.dma_start(pos1_sb[:], pos1)
         nc.sync.dma_start(pos2_sb[:], pos2)

@@ -194,23 +194,23 @@ def tile_moe_cap2_lin_bias_kernel(
             nc.vector.tensor_tensor(target, first, second, ADD)
 
         direct = block("direct", T)
-        got = [block("got%d" % i, n) for i, n in enumerate((256, 256, 128, 64))]
-        made = [block("made%d" % i, n) for i, n in enumerate((320, 256, 128))]
+        got = [block("got%d" % i, n) for i, n in enumerate((256, 192, 128, 128))]
+        made = [block("made%d" % i, n) for i, n in enumerate((256, 256, 128))]
         result = block("result", T)
         fetch(got[0][:], 0, 0, 256)
         weigh(direct[:], slots_of(1, 0, T), 1, 0, T)
-        weigh(made[0][:, :64], slots_of(0, 640, 64), 0, 640, 64)
-        fetch(got[1][:], 0, 256, 256)
+        fetch(got[1][:], 0, 256, 192)
         fetch(got[2][:], 0, 512, 128)
-        fetch(got[3][:], 0, 704, 64)
-        weigh(made[0][:, 64:], got[0][:], 0, 0, 256)
-        weigh(made[1][:], got[1][:], 0, 256, 256)
-        add(result[:, 0:256], direct[:, :256], made[0][:, 64:])
+        fetch(got[3][:], 0, 640, 128)
+        weigh(made[0][:], got[0][:], 0, 0, 256)
+        weigh(made[1][:, 192:], slots_of(0, 448, 64), 0, 448, 64)
+        weigh(made[1][:, :192], got[1][:], 0, 256, 192)
+        add(result[:, 0:256], direct[:, :256], made[0][:])
         nc.sync.dma_start(out=out[:, 0:256], in_=result[:, 0:256])
         weigh(made[2][:], got[2][:], 0, 512, 128)
-        weigh(made[0][:, 64:128], got[3][:], 0, 704, 64)
         add(result[:, 256:512], direct[:, 256:512], made[1][:])
         nc.sync.dma_start(out=out[:, 256:512], in_=result[:, 256:512])
+        weigh(made[0][:, :128], got[3][:], 0, 640, 128)
         add(result[:, 512:640], direct[:, 512:640], made[2][:])
         add(result[:, 640:768], direct[:, 640:768], made[0][:, :128])
         nc.sync.dma_start(out=out[:, 512:768], in_=result[:, 512:768])

from contextlib import ExitStack

import concourse.mybir as mybir

K, T, E, C, N = 1024, 768, 4, 256, 128
PAD = 32
P = 128
PACK = 4
SLOTS = E * C
FLOPS = 2 * K * N * SLOTS

F32 = mybir.dt.float32
BF16 = mybir.dt.bfloat16
I32 = mybir.dt.int32
U32 = mybir.dt.uint32
U16 = mybir.dt.uint16
U8 = mybir.dt.uint8
E4M3X4 = mybir.dt.float8_e4m3fn_x4
E2M1X4 = mybir.dt.float4_e2m1fn_x4

MULT = mybir.AluOpType.mult
ADD = mybir.AluOpType.add
IDENTITY = mybir.ActivationFunctionType.Identity
COPY = mybir.ActivationFunctionType.Copy

LOADS = ((0, 0, 512), (0, 512, 256), (1, 0, 256), (1, 256, 256), (1, 512, 256))
CHUNKS = (
    (0, 0, 256, 256),
    (0, 256, 256, 64),
    (1, 0, 256, 144),
    (2, 0, 256, 0),
    (3, 0, 256, 0),
    (4, 0, 256, 128),
)
GROUPS = ((0, 256), (256, 256), (512, 256), (768, 128), (896, 128))
SCALE_ROW = (4, 0)
BYTE_WINDOW = T
WORD_WINDOW = 1216
FIRST_BYTE = 128


def tile_moe_cap2_lin_bias_kernel(
    tc, xT, w8_words, w8_scales, w4_words, w4_scales, b, gate, offs, pos1, pos2, out
):
    nc = tc.nc
    with ExitStack() as ctx:
        lists = ctx.enter_context(tc.tile_pool(name="lists", bufs=1))
        keep = ctx.enter_context(tc.tile_pool(name="keep", bufs=1))
        psum = ctx.enter_context(tc.psum_pool(name="psum", bufs=1))

        free = {"next": FIRST_BYTE}

        def place(shape, dtype, size, name, align=64):
            count = 1
            for n in shape[1:]:
                count = count * n
            at = free["next"]
            free.update({"next": at + -(-count * size // 64) * 64})
            return keep.tile(shape, dtype, align_bytes=align, name=name, offset=at)

        offs_sb = lists.tile([P, SLOTS // 16], U16, align_bytes=256, name="offs_sb")
        pos1_sb = lists.tile([P, T // 16], U16, name="pos1_sb")
        pos2_sb = lists.tile([P, T // 16], U16, name="pos2_sb")

        s8 = place([P, E * N], U8, 1, "s8")
        s4 = place([P, E * N], U8, 1, "s4")
        nc.vector.memset(s8[:].bitcast(I32), 0)
        nc.gpsimd.memset(s4[:].bitcast(I32), 0)
        token_bytes = place([P, BYTE_WINDOW], U8, 1, "token_bytes")
        nc.vector.memset(token_bytes[:].bitcast(I32), 0)
        y = place([P, SLOTS + PAD], F32, 4, "y")
        nc.vector.memset(y[:, SLOTS:], 0.0)

        def load_scales(plane, scales, queue):
            view = plane[:].rearrange("p (e n) -> p e n", e=E)
            for q in range(4):
                queue.dma_start(
                    out=view[32 * q : 32 * q + 4, :, :].bitcast(I32),
                    in_=scales[:, 0, 4 * q : 4 * q + 4, :].rearrange("e q n -> q e n").bitcast(I32),
                )


        raws = []
        for i, (a, t0, n) in enumerate(LOADS):
            last_raw = free["next"]
            raw = place([P, PACK, n], F32, 4, "raw%d" % i, 256)
            rows = xT[a * 512 : (a + 1) * 512, t0 : t0 + n]
            nc.sync.dma_start(out=raw[:], in_=rows.rearrange("(p j) t -> p j t", j=PACK))
            raws.append(raw)
            if i == 1:
                nc.sync.dma_start(offs_sb[:], offs)

        w8 = place([P, E, 4 * N], U8, 1, "w8")
        nc.sync.dma_start(out=w8[:].bitcast(I32), in_=w8_words[:, 0].rearrange("e p n r -> p e (n r)").bitcast(I32))
        w4 = place([P, E, 2 * N], U8, 1, "w4")
        nc.sync.dma_start(out=w4[:].bitcast(I32), in_=w4_words[:, 0].rearrange("e p n -> p e n").bitcast(I32))
        load_scales(s8, w8_scales, nc.sync)
        load_scales(s4, w4_scales, nc.sync)
        bias = keep.tile([P, E], F32, align_bytes=64, name="bias", offset=0)
        nc.sync.dma_start(out=bias[:], in_=b)
        nc.sync.dma_start(pos1_sb[:], pos1)
        nc.sync.dma_start(pos2_sb[:], pos2)
        gates = [place([P, T], F32, 4, "gates%d" % which) for which in range(2)]
        for which in (1, 0):
            nc.sync.dma_start(out=gates[which][:], in_=gate[which])

        words = [place([P, (WORD_WINDOW, T)[a]], I32, 4, "words%d" % a) for a in range(2)]
        nc.vector.memset(words[0][:, T:], 0)
        slot_words = [place([P, (SLOTS - 128, SLOTS)[a]], U32, 4, "slot_words%d" % a) for a in range(2)]
        slot_bytes = place([P, SLOTS], U8, 1, "slot_bytes")

        grouped = [place([P, n, PACK], BF16, 2, "grouped%d" % i) for i, (a, t0, n, v) in enumerate(CHUNKS)]

        def cast(i):
            load, t0, n, v = CHUNKS[i]
            for copy, c0, c1 in ((nc.vector.tensor_copy, 0, v), (nc.scalar.copy, v, n)):
                if c0 < c1:
                    copy(
                        grouped[i][:, c0:c1, :].rearrange("p (c i) j -> p c j i", i=2),
                        raws[load][:, :, t0 + c0 : t0 + c1].rearrange("p j (c i) -> p c j i", i=2),
                    )

        def quantise(i):
            load, t0, n, v = CHUNKS[i]
            a, t0 = LOADS[load][0], LOADS[load][1] + t0
            nc.vector.quantize_mx(
                out=words[a][:, t0 : t0 + n].bitcast(E4M3X4),
                scales=token_bytes[SCALE_ROW[a] : P, t0 : t0 + n],
                in_=grouped[i][:].rearrange("p t j -> p (t j)"),
            )

        def gather(dst, src, s0, n, d0=0):
            nc.vector.tensor_copy(dst[:, s0 - d0 : s0 - d0 + n], src.indirect(offs_sb[:, s0 // 16 : (s0 + n) // 16]))

        cast(0)
        cast(1)
        quantise(0)
        cast(2)
        quantise(1)
        quantise(2)
        gather(slot_words[0], words[0][:].bitcast(U32), 0, 896)
        cast(3)
        quantise(3)
        cast(4)
        cast(5)
        quantise(4)
        quantise(5)
        late_words = keep.tile([P, 128], U32, align_bytes=64, name="late_words", offset=last_raw)
        gather(late_words, words[0][:, :T].bitcast(U32), 896, 128, 896)

        banks = [psum.tile([P, n], F32, name="bank%d" % g) for g, (s0, n) in enumerate(GROUPS)]

        def multiply(a, g):
            s0, n = GROUPS[g]
            e = s0 // C
            nc.tensor.matmul_mx(
                out=banks[g][:],
                lhsT=(w8[:, e, :].bitcast(E4M3X4), w4[:, e, :].bitcast(E2M1X4))[a],
                lhsT_scale=(s8, s4)[a][:, e * N : (e + 1) * N],
                rhs=(late_words[:] if (a, s0) == (0, 896) else slot_words[a][:, s0 : s0 + n]).bitcast(E4M3X4),
                rhs_scale=slot_bytes[SCALE_ROW[a] : P, s0 : s0 + n],
                start=(a == 0),
                stop=(a == 1),
            )

        for half in (0, 512):
            gather(slot_bytes, token_bytes[:], half, 512)
            for g, (s0, n) in enumerate(GROUPS):
                if half <= s0 < half + 512:
                    multiply(0, g)

        for g, (s0, n) in enumerate(GROUPS):
            gather(slot_words[1], words[1][:].bitcast(U32), s0, n)
            multiply(1, g)
            e = s0 // C
            cols = slice(s0, s0 + n)
            nc.scalar.activation(y[:, cols], banks[g][:], IDENTITY, bias=bias[:, e : e + 1], scale=1.0)

        choices = (pos1_sb, pos2_sb)

        def block(name, n):
            return place([P, n], F32, 4, name)

        def slots_of(which, t0, n):
            return y[:].indirect(choices[which][:, t0 // 16 : (t0 + n) // 16])

        def fetch(target, which, t0, n):
            nc.scalar.activation(target, slots_of(which, t0, n), COPY)

        def weigh(target, source, which, t0, n):
            nc.vector.tensor_tensor(target, source, gates[which][:, t0 : t0 + n], MULT)

        def add(target, first, second):
            nc.vector.tensor_tensor(target, first, second, ADD)

        direct = block("direct", T)
        got = [block("got%d" % i, n) for i, n in enumerate((256, 192, 128, 128))]
        made = [block("made%d" % i, n) for i, n in enumerate((256, 256, 128))]
        result = block("result", T)
        fetch(got[0][:], 0, 0, 256)
        weigh(direct[:], slots_of(1, 0, T), 1, 0, T)
        fetch(got[1][:], 0, 256, 192)
        fetch(got[2][:], 0, 512, 128)
        fetch(got[3][:], 0, 640, 128)
        weigh(made[0][:], got[0][:], 0, 0, 256)
        weigh(made[1][:, 192:], slots_of(0, 448, 64), 0, 448, 64)
        weigh(made[1][:, :192], got[1][:], 0, 256, 192)
        add(result[:, 0:256], direct[:, :256], made[0][:])
        nc.sync.dma_start(out=out[:, 0:256], in_=result[:, 0:256])
        weigh(made[2][:], got[2][:], 0, 512, 128)
        add(result[:, 256:512], direct[:, 256:512], made[1][:])
        nc.sync.dma_start(out=out[:, 256:512], in_=result[:, 256:512])
        weigh(made[0][:, :128], got[3][:], 0, 640, 128)
        add(result[:, 512:640], direct[:, 512:640], made[2][:])
        add(result[:, 640:768], direct[:, 640:768], made[0][:, :128])
        nc.sync.dma_start(out=out[:, 512:768], in_=result[:, 512:768])
